import numpy as np
import ml_dtypes


def mxq(x, axis, fmt="e4m3"):
    dtype, down = {"e4m3": (ml_dtypes.float8_e4m3fn, 7), "e5m2": (ml_dtypes.float8_e5m2, 14)}[fmt]
    v = np.moveaxis(np.asarray(x, np.float32).astype(ml_dtypes.bfloat16).astype(np.float64), axis, -1)
    blocks = v.reshape(v.shape[:-1] + (-1, 32))
    amax = np.abs(blocks).max(-1, keepdims=True)
    byte = np.maximum(np.where(amax > 0, np.frexp(amax)[1] - 1 + 127, 0) - down, 1)
    scale = np.exp2(byte - 127.0)
    codes = (blocks / scale).astype(np.float32).astype(dtype).astype(np.float64)
    return np.moveaxis((codes * scale).reshape(v.shape), -1, axis)


WIDE = False


def mx_kscale(k):
    if not WIDE:
        return np.ones(k)
    levels = np.array([30, -30])
    if k % 512:
        return np.exp2(np.random.permutation(np.resize(levels, k // 32))).repeat(32)
    a = np.empty((k // 512, 16))
    for p in range(k // 512):
        a[p, :8] = np.random.permutation(np.resize(levels, 8))
        for g in range(8):
            far = levels[np.abs(levels - a[p, g]) >= 10]
            a[p, g + 8] = far[np.random.randint(len(far))]
    return np.exp2(a.ravel()).repeat(32)


def f64(x):
    return np.asarray(x).astype(np.float64)


def striped(idx):
    return np.tile(idx.reshape(-1, 16).T, (8, 1)).astype(np.uint16)


def unstriped(offs):
    return offs[:16].T.reshape(-1).astype(np.int64)


E2M1 = np.array([0.0, 0.5, 1.0, 1.5, 2.0, 3.0, 4.0, 6.0, -0.0, -0.5, -1.0, -1.5, -2.0, -3.0, -4.0, -6.0])


def pack_weight(w, fmt):
    k, n = w.shape
    w = f64(np.asarray(w, np.float32).astype(ml_dtypes.bfloat16)).reshape(k // 32, 32, n)
    amax = np.abs(w).max(1)
    if fmt == "e4m3":
        byte = np.frexp(amax)[1] - 1 + 127 - 7
    elif fmt == "e5m2":
        byte = np.frexp(amax)[1] - 1 + 127 - 14
    else:
        mant, ex = np.frexp(amax / 6.0)
        byte = np.where(mant > 0.5, ex, ex - 1) + 127
    byte = np.clip(np.where(amax > 0, byte, 1), 1, 254)
    scaled = (w * np.exp2(127.0 - byte)[:, None, :]).reshape(k, n).astype(np.float32)
    by_word = np.ascontiguousarray(scaled.reshape(k // 512, 128, 4, n).transpose(0, 1, 3, 2))
    if fmt == "e4m3":
        words = by_word.astype(ml_dtypes.float8_e4m3fn).view(np.uint8)
    elif fmt == "e5m2":
        words = by_word.astype(ml_dtypes.float8_e5m2).view(np.uint8)
    else:
        c = by_word.astype(ml_dtypes.float4_e2m1fn).view(np.uint8) & 0xF
        words = (c[..., 0::2] | (c[..., 1::2] << 4)).reshape(k // 512, 128, 2 * n)
    return np.ascontiguousarray(words), np.ascontiguousarray(byte.astype(np.uint8).reshape(k // 512, 16, n))


def unpack_weight(words, scales, fmt):
    g, _, n = scales.shape
    words = np.ascontiguousarray(words).reshape(g, 128, n, -1)
    if fmt == "e4m3":
        vals = words.view(ml_dtypes.float8_e4m3fn).astype(np.float64)
    elif fmt == "e5m2":
        vals = words.view(ml_dtypes.float8_e5m2).astype(np.float64)
    else:
        nib = np.empty((g, 128, n, 4), np.uint8)
        nib[..., 0::2] = words & 0xF
        nib[..., 1::2] = words >> 4
        vals = E2M1[nib]
    vals = vals * np.repeat(np.exp2(scales.astype(np.float64) - 127.0), 8, axis=1)[..., None]
    return vals.transpose(0, 1, 3, 2).reshape(g * 512, n)


def sigmoid(v):
    return 1.0 / (1.0 + np.exp(-np.maximum(v, -700.0)))


def d_sigmoid(v):
    s = 1.0 / (1.0 + np.exp(-np.maximum(v, -700.0)))
    return s * (1.0 - s)


K, T, E, C, H, N = 128, 1536, 6, 512, 512, 512


def by_expert(wq, xq):
    return np.concatenate([wq[e].T @ xq[:, e * C:(e + 1) * C] for e in range(E)], axis=1)


def setup_inputs():
    n = np.random.standard_normal
    s = mx_kscale(N)[:, None]
    u = mx_kscale(H)
    first = np.random.permutation(np.repeat(np.arange(E), T // E))
    second = (first + 1 + np.random.permutation(np.repeat(np.arange(E - 1), -(-T // (E - 1)))[:T])) % E
    while np.bincount(second, minlength=E).max() != T // E:
        load = np.bincount(second, minlength=E); hi, lo = int(load.argmax()), int(load.argmin())
        t = np.flatnonzero((second == hi) & (first != lo))[0]; second[t] = lo
    slot_token = np.empty(E * C, np.int64); pos = np.empty((2, T), np.int64); fill = np.zeros(E, np.int64)
    place = np.stack([np.random.permutation(C) for _ in range(E)])
    for r, deal in enumerate((first, second)):
        for t in np.random.permutation(T):
            e = deal[t]; j = e * C + place[e, fill[e]]; fill[e] += 1; slot_token[j] = t; pos[r, t] = j
    g = np.random.uniform(0.2, 0.8, T)
    w_slot = np.empty(E * C); w_slot[pos[0]] = g; w_slot[pos[1]] = 1.0 - g
    dy = pack_weight(n((N, T)) * s, "e5m2")
    return {
        "dy_words": dy[0],
        "dy_scales": dy[1],
        "a1": n((H, E * C)).astype(np.float32),
        "a3": n((H, E * C)).astype(np.float32),
        "w2": (n((E, N, H)) / np.sqrt(N) / s[None] * u[None, None, :]).astype(np.float32),
        "w1": (n((E, H, K)) / np.sqrt(H) / u[None, :, None]).astype(np.float32),
        "w3": (n((E, H, K)) / np.sqrt(H) / u[None, :, None]).astype(np.float32),
        "gate": np.tile(w_slot, (H, 1)).astype(np.float32),
        "offs": striped(slot_token),
        "pos1": striped(pos[0]),
        "pos2": striped(pos[1]),
    }


def reference(dy_words, dy_scales, a1, a3, w2, w1, w3, gate, offs, pos1, pos2):
    idx = unstriped(offs)
    gq = unpack_weight(dy_words, dy_scales, "e5m2")[:, idx]
    dh = f64(gate) * by_expert(mxq(f64(w2), 1, "e4m3"), gq)
    da1 = dh * f64(a3) * d_sigmoid(f64(a1))
    da3 = dh * sigmoid(f64(a1))
    dx = by_expert(mxq(f64(w1), 1, "e4m3"), mxq(da1, 0, "e5m2")) + by_expert(mxq(f64(w3), 1, "e4m3"), mxq(da3, 0, "e5m2"))
    return dx[:, unstriped(pos1)] + dx[:, unstriped(pos2)]

@@ -1,0 +1,283 @@
+from contextlib import ExitStack
+
+import concourse.mybir as mybir
+from concourse.masks import make_identity
+
+K, T, E, C, H, N = 128, 1536, 6, 512, 512, 512
+SLOTS = E * C
+FLOPS = 2 * SLOTS * (N * H + 2 * H * K)
+BYTES = N * T + 16 * T + 4 * (2 * H * SLOTS + E * N * H + 2 * E * H * K + SLOTS + K * T) + 2 * 128 * (SLOTS + 2 * T) // 16
+
+F32 = mybir.dt.float32
+BF16 = mybir.dt.bfloat16
+I32 = mybir.dt.int32
+U32 = mybir.dt.uint32
+U16 = mybir.dt.uint16
+U8 = mybir.dt.uint8
+E4M3 = mybir.dt.float8_e4m3fn_x4
+E5M2 = mybir.dt.float8_e5m2_x4
+MULT = mybir.AluOpType.mult
+ADD = mybir.AluOpType.add
+SIGMOID = mybir.ActivationFunctionType.Sigmoid
+
+P = 128
+PACK = 4
+CHUNK = 128
+PER_EXPERT = C // CHUNK
+CHUNKS = SLOTS // CHUNK
+OUT_PIECES = (640, 512, 384)
+
+
+def tile_moe_bdx_glu_sigmoid_kernel(
+    tc, dy_words, dy_scales, a1, a3, w2, w1, w3, gate, offs, pos1, pos2, out
+):
+    nc = tc.nc
+    with ExitStack() as ctx:
+        held = ctx.enter_context(tc.tile_pool(name="held", bufs=1))
+        loads = ctx.enter_context(tc.tile_pool(name="loads", bufs=3))
+        work = ctx.enter_context(tc.tile_pool(name="work", bufs=2))
+        ring = ctx.enter_context(tc.tile_pool(name="ring", bufs=4))
+        psum = ctx.enter_context(tc.psum_pool(name="psum", bufs=2))
+
+        slot_list = held.tile([P, SLOTS // 16], U16, name="slot_list")
+        first_list = held.tile([P, T // 16], U16, name="first_list")
+        second_list = held.tile([P, T // 16], U16, name="second_list")
+        token_words = held.tile([P, T], I32, name="token_words", align_bytes=64)
+        token_scales = held.tile([P, T], U8, name="token_scales", align_bytes=64)
+        identity = held.tile([P, P], F32, name="identity")
+        gate_rows = held.tile([P, P], F32, name="gate_rows")
+        gate_cols = held.tile([P, CHUNKS], F32, name="gate_cols")
+        dx = held.tile([P, SLOTS], F32, name="dx")
+
+        t = {}
+
+        def load_a1(e):
+            t["a1", e] = loads.tile([P, PACK, C], F32, name="a1_rows")
+            nc.sync.dma_start(t["a1", e][:], a1[:, e * C : (e + 1) * C].rearrange("(p j) c -> p j c", j=PACK))
+
+        def load_a3(e):
+            t["a3", e] = loads.tile([P, PACK, C], F32, name="a3_rows")
+            nc.sync.dma_start(t["a3", e][:], a3[:, e * C : (e + 1) * C].rearrange("(p j) c -> p j c", j=PACK))
+
+        def load_w2(e):
+            t["w2", e] = loads.tile([P, PACK, H], F32, name="w2_rows")
+            nc.sync.dma_start(t["w2", e][:], w2[e].rearrange("(p j) i -> p j i", j=PACK))
+
+        def load_w13(e):
+            t["w13", e] = loads.tile([P, 2, PACK, K], F32, name="w13_rows")
+            for which, w in enumerate((w1, w3)):
+                nc.sync.dma_start(t["w13", e][:, which], w[e].rearrange("(p j) k -> p j k", j=PACK))
+
+        def gather_words(e):
+            t["gw", e] = work.tile([P, C], U32, name="slot_words", align_bytes=64, bufs=E)
+            nc.vector.tensor_copy(
+                t["gw", e][:], token_words[:].bitcast(U32).indirect(slot_list[:, e * C // 16 : (e + 1) * C // 16])
+            )
+
+        def gather_scales(e):
+            t["gs", e] = work.tile([P, C], U8, name="slot_scales", align_bytes=64, bufs=E)
+            nc.vector.tensor_copy(t["gs", e][:], token_scales[:].indirect(slot_list[:, e * C // 16 : (e + 1) * C // 16]))
+
+        def round_w2(e, q):
+            if q == 0:
+                t["w2b", e] = work.tile([P, H, PACK], BF16, name="w2_bf16", align_bytes=64)
+            cols = slice(q * CHUNK, (q + 1) * CHUNK)
+            nc.scalar.copy(
+                t["w2b", e][:, cols, :].rearrange("p (c i) j -> p c j i", i=4),
+                t["w2", e][:, :, cols].rearrange("p j (c i) -> p c j i", i=4),
+            )
+
+        def quantize_w2(e):
+            t["w2c", e] = work.tile([P, H], U32, name="w2_codes", align_bytes=64)
+            t["w2s", e] = work.tile([P, H], U8, name="w2_scales", align_bytes=64)
+            nc.vector.quantize_mx(t["w2c", e][:].bitcast(E4M3), t["w2s", e][:], t["w2b", e][:].rearrange("p i j -> p (i j)"))
+
+        def round_w13(e, which):
+            if which == 0:
+                t["w13b", e] = work.tile([P, 2, K, PACK], BF16, name="w13_bf16", align_bytes=64)
+            nc.scalar.copy(
+                t["w13b", e][:, which].rearrange("p (c i) j -> p c j i", i=4),
+                t["w13", e][:, which].rearrange("p j (c i) -> p c j i", i=4),
+            )
+
+        def quantize_w13(e):
+            t["w13c", e] = work.tile([P, 2 * K], U32, name="w13_codes", align_bytes=64)
+            t["w13s", e] = work.tile([P, 2 * K], U8, name="w13_scales", align_bytes=64)
+            nc.vector.quantize_mx(
+                t["w13c", e][:].bitcast(E4M3), t["w13s", e][:], t["w13b", e][:].rearrange("p w k j -> p (w k j)")
+            )
+
+        def where(g):
+            e, c = divmod(g, PER_EXPERT)
+            return e, slice(c * CHUNK, (c + 1) * CHUNK)
+
+        def turn_a1(g):
+            e, cols = where(g)
+            t["A", g] = psum.tile([P, PACK, P], F32, name="a1_turned")
+            for j in range(PACK):
+                nc.tensor.transpose(t["A", g][:, j, :], t["a1", e][:, j, cols], identity[:])
+
+        def multiply_w2(g):
+            e, cols = where(g)
+            t["B", g] = psum.tile([P, H], F32, name="dh_sums")
+            nc.tensor.matmul_mx(
+                t["B", g][:],
+                lhsT=t["gw", e][:, cols].bitcast(E5M2),
+                lhsT_scale=t["gs", e][:, cols],
+                rhs=t["w2c", e][:].bitcast(E4M3),
+                rhs_scale=t["w2s", e][:],
+                start=True,
+                stop=True,
+            )
+
+        def sigmoid_turned(g):
+            t["sT", g] = ring.tile([P, PACK, P], F32, name="sig_turned")
+            nc.scalar.activation(t["sT", g][:], t["A", g][:], SIGMOID)
+
+        def sigmoid_negated(g):
+            e, cols = where(g)
+            t["sm", g] = ring.tile([P, PACK, CHUNK], F32, name="sig_negated")
+            nc.scalar.activation(t["sm", g][:], t["a1", e][:, :, cols], SIGMOID, scale=-1.0)
+
+        def factor(g):
+            e, cols = where(g)
+            t["u", g] = ring.tile([P, PACK, CHUNK], F32, name="factor")
+            nc.vector.tensor_tensor(t["u", g][:], t["sm", g][:], t["a3", e][:, :, cols], MULT)
+
+        def da3_turned(g):
+            t["d3T", g] = ring.tile([P, PACK, P], F32, name="da3_turned")
+            nc.vector.scalar_tensor_tensor(
+                t["d3T", g][:],
+                t["B", g][:].rearrange("p (m j) -> p j m", j=PACK),
+                gate_cols[:, g : g + 1],
+                t["sT", g][:],
+                MULT,
+                MULT,
+            )
+
+        def turn_da3(g):
+            t["C", g] = psum.tile([P, PACK, CHUNK], F32, name="da3_back", bufs=3)
+            for j in range(PACK):
+                nc.tensor.transpose(t["C", g][:, j, :], t["d3T", g][:, j, :], identity[:])
+
+        def round_da1(g):
+            e, cols = where(g)
+            if g % PER_EXPERT == 0:
+                t["da", e] = work.tile([P, 2, C, PACK], BF16, name="da_bf16", align_bytes=64)
+            nc.vector.tensor_tensor(
+                t["da", e][:, 0, cols, :].rearrange("p (c i) j -> p c j i", i=2),
+                t["C", g][:].rearrange("p j (c i) -> p c j i", i=2),
+                t["u", g][:].rearrange("p j (c i) -> p c j i", i=2),
+                MULT,
+            )
+
+        def round_da3(g):
+            e, cols = where(g)
+            nc.scalar.copy(t["da", e][:, 1, cols, :], t["C", g][:].rearrange("p j c -> p c j"))
+
+        def quantize_da(e, first, last):
+            if first == 0:
+                t["dac", e] = work.tile([P, 2 * C], U32, name="da_codes", align_bytes=64)
+                t["das", e] = work.tile([P, 2 * C], U8, name="da_scales", align_bytes=64)
+            for which in range(2):
+                part = slice(which * C + first, which * C + last)
+                nc.vector.quantize_mx(
+                    t["dac", e][:, part].bitcast(E5M2),
+                    t["das", e][:, part],
+                    t["da", e][:, which, first:last, :].rearrange("p c j -> p (c j)"),
+                )
+
+        def multiply_w13(e):
+            t["D", e] = psum.tile([P, C], F32, name="dx_sums", bufs=1)
+            for which in range(2):
+                kcols = slice(which * K, (which + 1) * K)
+                half = slice(which * C, (which + 1) * C)
+                nc.tensor.matmul_mx(
+                    t["D", e][:],
+                    lhsT=t["w13c", e][:, kcols].bitcast(E4M3),
+                    lhsT_scale=t["w13s", e][:, kcols],
+                    rhs=t["dac", e][:, half].bitcast(E5M2),
+                    rhs_scale=t["das", e][:, half],
+                    start=(which == 0),
+                    stop=(which == 1),
+                )
+
+        def keep_dx(e):
+            nc.scalar.copy(dx[:, e * C : (e + 1) * C], t["D", e][:])
+
+        make_identity(nc, identity[:])
+        nc.vector.memset(token_scales[:].bitcast(I32), 0)
+        nc.sync.dma_start(slot_list[:], offs)
+        nc.sync.dma_start(token_words[:], dy_words[0].rearrange("p t d -> p (t d)").bitcast(I32))
+        for q in range(4):
+            nc.sync.dma_start(token_scales[32 * q : 32 * q + 4, :].bitcast(I32), dy_scales[0, 4 * q : 4 * q + 4, :].bitcast(I32))
+        load_a1(0)
+        load_w2(0)
+        nc.sync.dma_start(gate_rows[:], gate.rearrange("h (r c) -> (h r) c", c=P)[0:P, :])
+        load_a3(0)
+        load_w13(0)
+        nc.sync.dma_start(first_list[:], pos1)
+        nc.sync.dma_start(second_list[:], pos2)
+        gate_turned = psum.tile([P, C], F32, name="dx_sums", bufs=1)
+        nc.tensor.transpose(gate_turned[:, 0:P], gate_rows[:], identity[:])
+        nc.vector.tensor_copy(gate_cols[:], gate_turned[:, 0:CHUNKS])
+
+        def live(g):
+            return 0 <= g < CHUNKS
+
+        for s in range(-6, CHUNKS + 3):
+            e_load, r_load = divmod(s + 10, PER_EXPERT)
+            if 1 <= e_load < E:
+                (load_w2, load_a1, load_a3, load_w13)[r_load](e_load)
+            if live(s - 1):
+                turn_da3(s - 1)
+            if live(s + 1):
+                turn_a1(s + 1)
+                multiply_w2(s + 1)
+            if live(s):
+                da3_turned(s)
+            if live(s + 1):
+                sigmoid_turned(s + 1)
+                sigmoid_negated(s + 1)
+            if live(s):
+                factor(s)
+            if live(s - 1):
+                round_da1(s - 1)
+                round_da3(s - 1)
+            e_w2, r_w2 = divmod(s + 6, PER_EXPERT)
+            if 0 <= e_w2 < E:
+                round_w2(e_w2, r_w2)
+                if r_w2 == 0:
+                    gather_words(e_w2)
+                if r_w2 == 1:
+                    gather_scales(e_w2)
+            e_q, r_q = divmod(s + 2, PER_EXPERT)
+            if r_q == 0 and 0 <= e_q < E:
+                quantize_w2(e_q)
+            e_now, r_now = divmod(s, PER_EXPERT)
+            if 0 <= e_now < E and r_now < 2:
+                round_w13(e_now, r_now)
+            if 0 <= e_now < E and r_now == 3:
+                quantize_w13(e_now)
+            e_done, r_done = divmod(s - 5, PER_EXPERT)
+            if s == CHUNKS - 1:
+                quantize_da(E - 1, 0, 2 * CHUNK)
+            if s == CHUNKS:
+                quantize_da(E - 1, 2 * CHUNK, 3 * CHUNK)
+            if 0 <= e_done < E and r_done == 0:
+                quantize_da(e_done, 3 * CHUNK if e_done == E - 1 else 0, C)
+                multiply_w13(e_done)
+            if 0 <= e_done < E and r_done == 1:
+                keep_dx(e_done)
+
+        start = 0
+        for width in OUT_PIECES:
+            cols = slice(start // 16, (start + width) // 16)
+            first = work.tile([P, width], F32, name="first", bufs=3)
+            second = work.tile([P, width], F32, name="second", bufs=3)
+            total = work.tile([P, width], F32, name="total", bufs=3)
+            nc.vector.tensor_copy(first[:], dx[:].indirect(first_list[:, cols]))
+            nc.vector.tensor_copy(second[:], dx[:].indirect(second_list[:, cols]))
+            nc.vector.tensor_tensor(total[:], first[:], second[:], ADD)
+            nc.sync.dma_start(out[:, start : start + width], total[:])
+            start += width

@@ -3,6 +3,7 @@ from contextlib import ExitStack
 import concourse.mybir as mybir
 from concourse.masks import make_identity
 
+O = {'fstep': 0, 'dtag': 'dh_sums', 'smb': 2, 'la': 2, 'addG': False, 'gw': 3, 'gs': 1, 'c13': 'G', 'w13b': 1, 'w13c': 2, 'w2c': 2, 'w2b': 2, 'ub': 2, 'host': 'da', 'w2V': ((0, 1),), 'ps': (2, 3, 3), 'sT': 2, 'd3': 2, 'un': 4, 'uV': (), 'scq': 'Q', 'head': 'offs a1a words scales w2 gate a3 a1b', 'lead': {'w': -1.5, 'a': 1, 'b': 2, 'x': 3}, 'pos': 6, 'q13': 1, 'r13': -3, 'qw2': -4, 'fac': -1, 'qdafirst': True, 'sm': (-7, -6), 'rw2': (-4, -4), 'gat': (-3, -2), 'gfirst': True, 'out': (640, 512, 384), 'pin': {'gw': ('d3', -6, 1), 'gs': ('d3', -4, 1), 'w2s': ('sT', -5, 2), 'w13s': ('sT', 1, 0)}}
 K, T, E, C, H, N = 128, 1536, 6, 512, 512, 512
 SLOTS = E * C
 FLOPS = 2 * SLOTS * (N * H + 2 * H * K)
@@ -23,9 +24,10 @@ SIGMOID = mybir.ActivationFunctionType.Sigmoid
 P = 128
 PACK = 4
 CHUNK = 128
+HALF = 256
 PER_EXPERT = C // CHUNK
 CHUNKS = SLOTS // CHUNK
-OUT_PIECES = (640, 512, 384)
+OUT_PIECES = O["out"]
 
 
 def tile_moe_bdx_glu_sigmoid_kernel(
@@ -36,7 +38,7 @@ def tile_moe_bdx_glu_sigmoid_kernel(
         held = ctx.enter_context(tc.tile_pool(name="held", bufs=1))
         loads = ctx.enter_context(tc.tile_pool(name="loads", bufs=3))
         work = ctx.enter_context(tc.tile_pool(name="work", bufs=2))
-        ring = ctx.enter_context(tc.tile_pool(name="ring", bufs=4))
+        ring = ctx.enter_context(tc.tile_pool(name="ring", bufs=3))
         psum = ctx.enter_context(tc.psum_pool(name="psum", bufs=2))
 
         slot_list = held.tile([P, SLOTS // 16], U16, name="slot_list")
@@ -50,18 +52,34 @@ def tile_moe_bdx_glu_sigmoid_kernel(
         dx = held.tile([P, SLOTS], F32, name="dx")
 
         t = {}
+        pins = {}
+        for kind, (src, r, first) in O["pin"].items():
+            for e in range(first, E):
+                if 0 <= PER_EXPERT * e + r < CHUNKS:
+                    pins[src, PER_EXPERT * e + r] = (kind, e)
+        pinned = set(pins.values())
 
-        def load_a1(e):
-            t["a1", e] = loads.tile([P, PACK, C], F32, name="a1_rows")
-            nc.sync.dma_start(t["a1", e][:], a1[:, e * C : (e + 1) * C].rearrange("(p j) c -> p j c", j=PACK))
+        def place(pool, shape, dtype, name, key, bufs):
+            if key in pins:
+                key = pins[key]
+            if key in pinned:
+                return held.tile(shape, dtype, name=name, tag="pin_%s%d" % (key[0], key[1] % (3 if key[0] in ("gw", "gs") else 2)), align_bytes=64)
+            return pool.tile(shape, dtype, name=name, align_bytes=64, bufs=bufs)
+
+        def load_a1(e, first=0, last=C):
+            if first == 0:
+                t["a1", e] = loads.tile([P, PACK, C], F32, name="a1_rows")
+            rows = a1[:, e * C + first : e * C + last].rearrange("(p j) c -> p j c", j=PACK)
+            nc.sync.dma_start(t["a1", e][:, :, first:last], rows)
 
         def load_a3(e):
             t["a3", e] = loads.tile([P, PACK, C], F32, name="a3_rows")
             nc.sync.dma_start(t["a3", e][:], a3[:, e * C : (e + 1) * C].rearrange("(p j) c -> p j c", j=PACK))
 
-        def load_w2(e):
-            t["w2", e] = loads.tile([P, PACK, H], F32, name="w2_rows")
-            nc.sync.dma_start(t["w2", e][:], w2[e].rearrange("(p j) i -> p j i", j=PACK))
+        def load_w2(e, first=0, last=H):
+            if first == 0:
+                t["w2", e] = loads.tile([P, PACK, H], F32, name="w2_rows")
+            nc.sync.dma_start(t["w2", e][:, :, first:last], w2[e][:, first:last].rearrange("(p j) i -> p j i", j=PACK))
 
         def load_w13(e):
             t["w13", e] = loads.tile([P, 2, PACK, K], F32, name="w13_rows")
@@ -69,43 +87,57 @@ def tile_moe_bdx_glu_sigmoid_kernel(
                 nc.sync.dma_start(t["w13", e][:, which], w[e].rearrange("(p j) k -> p j k", j=PACK))
 
         def gather_words(e):
-            t["gw", e] = work.tile([P, C], U32, name="slot_words", align_bytes=64, bufs=E)
+            t["gw", e] = place(work, [P, C], U32, "slot_words", ("gw", e), O["gw"])
             nc.vector.tensor_copy(
                 t["gw", e][:], token_words[:].bitcast(U32).indirect(slot_list[:, e * C // 16 : (e + 1) * C // 16])
             )
 
         def gather_scales(e):
-            t["gs", e] = work.tile([P, C], U8, name="slot_scales", align_bytes=64, bufs=E)
+            t["gs", e] = place(work, [P, C], U8, "slot_scales", ("gs", e), O["gs"])
             nc.vector.tensor_copy(t["gs", e][:], token_scales[:].indirect(slot_list[:, e * C // 16 : (e + 1) * C // 16]))
 
-        def round_w2(e, q):
-            if q == 0:
-                t["w2b", e] = work.tile([P, H, PACK], BF16, name="w2_bf16", align_bytes=64)
-            cols = slice(q * CHUNK, (q + 1) * CHUNK)
-            nc.scalar.copy(
-                t["w2b", e][:, cols, :].rearrange("p (c i) j -> p c j i", i=4),
-                t["w2", e][:, :, cols].rearrange("p j (c i) -> p c j i", i=4),
+        def round_w2(e, half):
+            if half == 0 and O["host"] == "w2":
+                t["u", e] = work.tile([P, PACK, C], F32, name="w2_then_factor", align_bytes=64, bufs=3)
+                t["w2b", e] = t["u", e][:, 0:2, :].rearrange("p j c -> p (j c)").bitcast(BF16)
+            elif half == 0:
+                t["w2b", e] = work.tile([P, H * PACK], BF16, name="w2_bf16", align_bytes=64, bufs=O["w2b"])[:]
+            staged = t["w2b", e].rearrange("p (c i j) -> p c j i", i=4, j=PACK)
+            (nc.vector.tensor_copy if (e, half) in O["w2V"] else nc.scalar.copy)(
+                staged[:, half * (128 // len(O["rw2"])) : (half + 1) * (128 // len(O["rw2"]))],
+                t["w2", e][:, :, half * (H // len(O["rw2"])) : (half + 1) * (H // len(O["rw2"]))].rearrange("p j (c i) -> p c j i", i=4),
             )
 
         def quantize_w2(e):
-            t["w2c", e] = work.tile([P, H], U32, name="w2_codes", align_bytes=64)
-            t["w2s", e] = work.tile([P, H], U8, name="w2_scales", align_bytes=64)
-            nc.vector.quantize_mx(t["w2c", e][:].bitcast(E4M3), t["w2s", e][:], t["w2b", e][:].rearrange("p i j -> p (i j)"))
+            t["w2c", e] = work.tile([P, H], U32, name="w2_codes", align_bytes=64, bufs=O["w2c"])
+            t["w2s", e] = place(work, [P, H], U8, "w2_scales", ("w2s", e), O["w2c"])
+            nc.vector.quantize_mx(t["w2c", e][:].bitcast(E4M3), t["w2s", e][:], t["w2b", e])
 
-        def round_w13(e, which):
-            if which == 0:
-                t["w13b", e] = work.tile([P, 2, K, PACK], BF16, name="w13_bf16", align_bytes=64)
-            nc.scalar.copy(
-                t["w13b", e][:, which].rearrange("p (c i) j -> p c j i", i=4),
-                t["w13", e][:, which].rearrange("p j (c i) -> p c j i", i=4),
-            )
+        def round_w13(e):
+            if O["c13"] == "G":
+                t["w13b", e] = t["sm", e][:, 0, :].bitcast(BF16)
+                for which in range(2):
+                    nc.gpsimd.tensor_scalar(
+                        t["w13b", e][:, which * C : (which + 1) * C].rearrange("p (k j) -> p k j", j=PACK),
+                        t["w13", e][:, which].rearrange("p j k -> p k j"),
+                        1.0,
+                        0.0,
+                        MULT,
+                        ADD,
+                    )
+            else:
+                t["w13b", e] = work.tile([P, 2 * K * PACK], BF16, name="w13_bf16", align_bytes=64, bufs=O["w13b"])[:]
+                a = t["w13b", e].rearrange("p (w c i j) -> p w c j i", w=2, i=4, j=PACK)
+                b = t["w13", e][:].rearrange("p w j (c i) -> p w c j i", i=4)
+                if O["c13"] == "S":
+                    nc.scalar.copy(a, b)
+                else:
+                    nc.vector.tensor_copy(a, b)
 
         def quantize_w13(e):
-            t["w13c", e] = work.tile([P, 2 * K], U32, name="w13_codes", align_bytes=64)
-            t["w13s", e] = work.tile([P, 2 * K], U8, name="w13_scales", align_bytes=64)
-            nc.vector.quantize_mx(
-                t["w13c", e][:].bitcast(E4M3), t["w13s", e][:], t["w13b", e][:].rearrange("p w k j -> p (w k j)")
-            )
+            t["w13c", e] = work.tile([P, 2 * K], U32, name="w13_codes", align_bytes=64, bufs=O["w13c"])
+            t["w13s", e] = place(work, [P, 2 * K], U8, "w13_scales", ("w13s", e), O["w13c"])
+            nc.vector.quantize_mx(t["w13c", e][:].bitcast(E4M3), t["w13s", e][:], t["w13b", e])
 
         def where(g):
             e, c = divmod(g, PER_EXPERT)
@@ -113,13 +145,13 @@ def tile_moe_bdx_glu_sigmoid_kernel(
 
         def turn_a1(g):
             e, cols = where(g)
-            t["A", g] = psum.tile([P, PACK, P], F32, name="a1_turned")
+            t["A", g] = psum.tile([P, PACK, P], F32, name="a1_turned", bufs=O["ps"][0])
             for j in range(PACK):
                 nc.tensor.transpose(t["A", g][:, j, :], t["a1", e][:, j, cols], identity[:])
 
         def multiply_w2(g):
             e, cols = where(g)
-            t["B", g] = psum.tile([P, H], F32, name="dh_sums")
+            t["B", g] = psum.tile([P, H], F32, name="dh_sums", bufs=O["ps"][1])
             nc.tensor.matmul_mx(
                 t["B", g][:],
                 lhsT=t["gw", e][:, cols].bitcast(E5M2),
@@ -131,21 +163,33 @@ def tile_moe_bdx_glu_sigmoid_kernel(
             )
 
         def sigmoid_turned(g):
-            t["sT", g] = ring.tile([P, PACK, P], F32, name="sig_turned")
+            t["sT", g] = place(ring, [P, PACK, P], F32, "sig_turned", ("sT", g), O["sT"])
             nc.scalar.activation(t["sT", g][:], t["A", g][:], SIGMOID)
 
-        def sigmoid_negated(g):
-            e, cols = where(g)
-            t["sm", g] = ring.tile([P, PACK, CHUNK], F32, name="sig_negated")
-            nc.scalar.activation(t["sm", g][:], t["a1", e][:, :, cols], SIGMOID, scale=-1.0)
+        def sigmoid_negated(e, half):
+            if half == 0:
+                t["sm", e] = work.tile([P, PACK, C], F32, name="sig_negated", align_bytes=64, bufs=O["smb"])
+            cols = slice(half * (C // len(O["sm"])), (half + 1) * (C // len(O["sm"])))
+            nc.scalar.activation(t["sm", e][:, :, cols], t["a1", e][:, :, cols], SIGMOID, scale=-1.0)
 
-        def factor(g):
-            e, cols = where(g)
-            t["u", g] = ring.tile([P, PACK, CHUNK], F32, name="factor")
-            nc.vector.tensor_tensor(t["u", g][:], t["sm", g][:], t["a3", e][:, :, cols], MULT)
+        def factor(e, parts):
+            n = O["un"]
+            if 0 not in parts:
+                pass
+            elif O["host"] == "da":
+                if e < 2:
+                    t["u", e] = held.tile([P, PACK, C], F32, name="da_then_factor", tag="zone%d" % ((e - 2) % 3), align_bytes=64)
+                else:
+                    t["u", e] = t["Z", e - 2]
+            elif O["host"] == "none":
+                t["u", e] = work.tile([P, PACK, C], F32, name="factor", align_bytes=64, bufs=O["ub"])
+            for part in parts:
+                cols = slice(part * C // n, (part + 1) * C // n)
+                eng = nc.vector if (e, part) in O["uV"] else nc.gpsimd
+                eng.tensor_tensor(t["u", e][:, :, cols], t["sm", e][:, :, cols], t["a3", e][:, :, cols], MULT)
 
         def da3_turned(g):
-            t["d3T", g] = ring.tile([P, PACK, P], F32, name="da3_turned")
+            t["d3T", g] = place(ring, [P, PACK, P], F32, "da3_turned", ("d3", g), O["d3"])
             nc.vector.scalar_tensor_tensor(
                 t["d3T", g][:],
                 t["B", g][:].rearrange("p (m j) -> p j m", j=PACK),
@@ -156,18 +200,22 @@ def tile_moe_bdx_glu_sigmoid_kernel(
             )
 
         def turn_da3(g):
-            t["C", g] = psum.tile([P, PACK, CHUNK], F32, name="da3_back", bufs=3)
+            t["C", g] = psum.tile([P, PACK, CHUNK], F32, name="da3_back", bufs=O["ps"][2])
             for j in range(PACK):
                 nc.tensor.transpose(t["C", g][:, j, :], t["d3T", g][:, j, :], identity[:])
 
         def round_da1(g):
             e, cols = where(g)
             if g % PER_EXPERT == 0:
-                t["da", e] = work.tile([P, 2, C, PACK], BF16, name="da_bf16", align_bytes=64)
+                if O["host"] == "da":
+                    t["Z", e] = held.tile([P, PACK, C], F32, name="da_then_factor", tag="zone%d" % (e % 3), align_bytes=64)
+                    t["da", e] = t["Z", e][:].rearrange("p j c -> p (j c)").bitcast(BF16).rearrange("p (w c j) -> p w c j", w=2, j=PACK)
+                else:
+                    t["da", e] = work.tile([P, 2, C, PACK], BF16, name="da_bf16", align_bytes=64)
             nc.vector.tensor_tensor(
                 t["da", e][:, 0, cols, :].rearrange("p (c i) j -> p c j i", i=2),
                 t["C", g][:].rearrange("p j (c i) -> p c j i", i=2),
-                t["u", g][:].rearrange("p j (c i) -> p c j i", i=2),
+                t["u", e][:, :, cols].rearrange("p j (c i) -> p c j i", i=2),
                 MULT,
             )
 
@@ -179,6 +227,9 @@ def tile_moe_bdx_glu_sigmoid_kernel(
             if first == 0:
                 t["dac", e] = work.tile([P, 2 * C], U32, name="da_codes", align_bytes=64)
                 t["das", e] = work.tile([P, 2 * C], U8, name="da_scales", align_bytes=64)
+            if last - first == C:
+                nc.vector.quantize_mx(t["dac", e][:].bitcast(E5M2), t["das", e][:], t["da", e][:].rearrange("p w c j -> p (w c j)"))
+                return
             for which in range(2):
                 part = slice(which * C + first, which * C + last)
                 nc.vector.quantize_mx(
@@ -188,7 +239,7 @@ def tile_moe_bdx_glu_sigmoid_kernel(
                 )
 
         def multiply_w13(e):
-            t["D", e] = psum.tile([P, C], F32, name="dx_sums", bufs=1)
+            t["D", e] = psum.tile([P, C], F32, name="dx_sums", tag=O["dtag"], bufs=dict(dx_sums=1, a1_turned=O["ps"][0], dh_sums=O["ps"][1], da3_back=O["ps"][2])[O["dtag"]])
             for which in range(2):
                 kcols = slice(which * K, (which + 1) * K)
                 half = slice(which * C, (which + 1) * C)
@@ -207,77 +258,111 @@ def tile_moe_bdx_glu_sigmoid_kernel(
 
         make_identity(nc, identity[:])
         nc.vector.memset(token_scales[:].bitcast(I32), 0)
-        nc.sync.dma_start(slot_list[:], offs)
-        nc.sync.dma_start(token_words[:], dy_words[0].rearrange("p t d -> p (t d)").bitcast(I32))
-        for q in range(4):
-            nc.sync.dma_start(token_scales[32 * q : 32 * q + 4, :].bitcast(I32), dy_scales[0, 4 * q : 4 * q + 4, :].bitcast(I32))
-        load_a1(0)
-        load_w2(0)
-        nc.sync.dma_start(gate_rows[:], gate.rearrange("h (r c) -> (h r) c", c=P)[0:P, :])
-        load_a3(0)
-        load_w13(0)
-        nc.sync.dma_start(first_list[:], pos1)
-        nc.sync.dma_start(second_list[:], pos2)
-        gate_turned = psum.tile([P, C], F32, name="dx_sums", bufs=1)
+        def load_scales():
+            for q in range(4):
+                (nc.scalar if O["scq"] == "S" else nc.sync).dma_start(token_scales[32 * q : 32 * q + 4, :].bitcast(I32), dy_scales[0, 4 * q : 4 * q + 4, :].bitcast(I32))
+
+        head = dict(
+            offs=lambda: nc.sync.dma_start(slot_list[:], offs),
+            words=lambda: nc.sync.dma_start(token_words[:], dy_words[0].rearrange("p t d -> p (t d)").bitcast(I32)),
+            scales=load_scales,
+            a1a=lambda: load_a1(0, 0, HALF),
+            a1b=lambda: load_a1(0, HALF, C),
+            a1=lambda: load_a1(0),
+            w2a=lambda: load_w2(0, 0, HALF),
+            w2b=lambda: load_w2(0, HALF, H),
+            w2=lambda: load_w2(0),
+            gate=lambda: nc.sync.dma_start(gate_rows[:], gate.rearrange("h (r c) -> (h r) c", c=P)[0:P, :]),
+            a3=lambda: load_a3(0),
+            w13=lambda: load_w13(0),
+        )
+        done = set()
+        for key in O["head"].split():
+            head[key]()
+            done.add((dict(a1="a", a1a="a", w2="w", w2a="w", a3="b", w13="x").get(key), 0))
+        gate_turned = psum.tile([P, C], F32, name="dx_sums", tag=O["dtag"], bufs=dict(dx_sums=1, a1_turned=O["ps"][0], dh_sums=O["ps"][1], da3_back=O["ps"][2])[O["dtag"]])
         nc.tensor.transpose(gate_turned[:, 0:P], gate_rows[:], identity[:])
         nc.vector.tensor_copy(gate_cols[:], gate_turned[:, 0:CHUNKS])
+
+        order = sorted(((k, e) for e in range(E) for k in "wabx" if (k, e) not in done), key=lambda x: 4 * x[1] + O["lead"][x[0]])
 
         def live(g):
             return 0 <= g < CHUNKS
 
-        for s in range(-6, CHUNKS + 3):
-            e_load, r_load = divmod(s + 10, PER_EXPERT)
-            if 1 <= e_load < E:
-                (load_w2, load_a1, load_a3, load_w13)[r_load](e_load)
+        for s in range(-12, CHUNKS + 3):
+            if s + 12 < len(order):
+                kind, e_load = order[s + 12]
+                dict(a=load_a1, w=load_w2, b=load_a3, x=load_w13)[kind](e_load)
+            if s == O["pos"]:
+                nc.sync.dma_start(first_list[:], pos1)
+                nc.sync.dma_start(second_list[:], pos2)
             if live(s - 1):
                 turn_da3(s - 1)
+            if live(s + O["la"]):
+                turn_a1(s + O["la"])
             if live(s + 1):
-                turn_a1(s + 1)
                 multiply_w2(s + 1)
             if live(s):
                 da3_turned(s)
-            if live(s + 1):
-                sigmoid_turned(s + 1)
-                sigmoid_negated(s + 1)
-            if live(s):
-                factor(s)
+            if live(s + O["la"]):
+                sigmoid_turned(s + O["la"])
             if live(s - 1):
                 round_da1(s - 1)
                 round_da3(s - 1)
-            e_w2, r_w2 = divmod(s + 6, PER_EXPERT)
-            if 0 <= e_w2 < E:
-                round_w2(e_w2, r_w2)
-                if r_w2 == 0:
-                    gather_words(e_w2)
-                if r_w2 == 1:
-                    gather_scales(e_w2)
-            e_q, r_q = divmod(s + 2, PER_EXPERT)
-            if r_q == 0 and 0 <= e_q < E:
-                quantize_w2(e_q)
-            e_now, r_now = divmod(s, PER_EXPERT)
-            if 0 <= e_now < E and r_now < 2:
-                round_w13(e_now, r_now)
-            if 0 <= e_now < E and r_now == 3:
-                quantize_w13(e_now)
-            e_done, r_done = divmod(s - 5, PER_EXPERT)
             if s == CHUNKS - 1:
                 quantize_da(E - 1, 0, 2 * CHUNK)
             if s == CHUNKS:
                 quantize_da(E - 1, 2 * CHUNK, 3 * CHUNK)
-            if 0 <= e_done < E and r_done == 0:
-                quantize_da(e_done, 3 * CHUNK if e_done == E - 1 else 0, C)
-                multiply_w13(e_done)
-            if 0 <= e_done < E and r_done == 1:
-                keep_dx(e_done)
+            for e in range(E):
+                r = s - PER_EXPERT * e
+                if r == 5 and O["qdafirst"]:
+                    quantize_da(e, 3 * CHUNK if e == E - 1 else 0, C)
+                    multiply_w13(e)
+                if r == 6:
+                    keep_dx(e)
+            for e in range(E):
+                r = s - PER_EXPERT * e
+                if r == O["q13"]:
+                    quantize_w13(e)
+                if r == O["r13"] and O["c13"] != "G":
+                    round_w13(e)
+                for half in range(len(O["sm"])):
+                    if r == O["sm"][half]:
+                        sigmoid_negated(e, half)
+                for half in range(len(O["rw2"])):
+                    if r == O["rw2"][half]:
+                        round_w2(e, half)
+                if r == O["gat"][0] and O["gfirst"]:
+                    gather_words(e)
+                if r == O["gat"][1] and O["gfirst"]:
+                    gather_scales(e)
+                if r == O["qw2"]:
+                    quantize_w2(e)
+            for e in range(E):
+                r = s - PER_EXPERT * e
+                if r == 5 and not O["qdafirst"]:
+                    quantize_da(e, 3 * CHUNK if e == E - 1 else 0, C)
+                    multiply_w13(e)
+            for e in range(E):
+                r = s - PER_EXPERT * e
+                parts = [q for q in range(O["un"]) if r == O["fac"] + q * O["fstep"]]
+                if parts:
+                    factor(e, parts)
+                    if O["c13"] == "G" and O["un"] - 1 in parts:
+                        round_w13(e)
+                if r == O["gat"][0] and not O["gfirst"]:
+                    gather_words(e)
+                if r == O["gat"][1] and not O["gfirst"]:
+                    gather_scales(e)
 
         start = 0
         for width in OUT_PIECES:
             cols = slice(start // 16, (start + width) // 16)
-            first = work.tile([P, width], F32, name="first", bufs=3)
-            second = work.tile([P, width], F32, name="second", bufs=3)
+            first = work.tile([P, width], F32, name="first")
+            second = work.tile([P, width], F32, name="second")
             total = work.tile([P, width], F32, name="total", bufs=3)
             nc.vector.tensor_copy(first[:], dx[:].indirect(first_list[:, cols]))
             nc.vector.tensor_copy(second[:], dx[:].indirect(second_list[:, cols]))
-            nc.vector.tensor_tensor(total[:], first[:], second[:], ADD)
+            (nc.gpsimd if O["addG"] and start + width < T else nc.vector).tensor_tensor(total[:], first[:], second[:], ADD)
             nc.sync.dma_start(out[:, start : start + width], total[:])
             start += width

@@ -3,7 +3,7 @@ from contextlib import ExitStack
 import concourse.mybir as mybir
 from concourse.masks import make_identity
 
-O = {'fstep': 0, 'dtag': 'dh_sums', 'smb': 2, 'la': 2, 'addG': False, 'gw': 3, 'gs': 1, 'c13': 'G', 'w13b': 1, 'w13c': 2, 'w2c': 2, 'w2b': 2, 'ub': 2, 'host': 'da', 'w2V': ((0, 1),), 'ps': (2, 3, 3), 'sT': 2, 'd3': 2, 'un': 4, 'uV': (), 'scq': 'Q', 'head': 'offs a1a words scales w2 gate a3 a1b', 'lead': {'w': -1.5, 'a': 1, 'b': 2, 'x': 3}, 'pos': 6, 'q13': 1, 'r13': -3, 'qw2': -4, 'fac': -1, 'qdafirst': True, 'sm': (-7, -6), 'rw2': (-4, -4), 'gat': (-3, -2), 'gfirst': True, 'out': (640, 512, 384), 'pin': {'gw': ('d3', -6, 1), 'gs': ('d3', -4, 1), 'w2s': ('sT', -5, 2), 'w13s': ('sT', 1, 0)}}
+O = {'slope': {}, 'dup': (23,), 'duptag': 'da3_back', 'dupb': 2, 'pair': False, 'lm': 1, 'fstep': 0, 'dtag': 'dx_sums', 'smb': 2, 'la': 2, 'addG': False, 'gw': 2, 'gs': 3, 'c13': 'SSSSSS', 'w13b': 1, 'w13c': 2, 'w2c': 1, 'w2b': 2, 'ub': 3, 'host': 'da', 'w2V': ((0, 1), (1, 0), (2, 0), (4, 0), (5, 1)), 'ps': (2, 2, 3), 'sT': 3, 'd3': 2, 'un': 4, 'uV': ((0, 0), (0, 3), (1, 1), (1, 3), (2, 1), (2, 2), (2, 3), (5, 1)), 'scq': 'Q', 'head': 'offs words scales a1 w2 gate', 'lead': {'w': 0, 'a': 1, 'b': 2, 'x': 5.5}, 'pos': 6, 'q13': 4, 'r13': 2, 'qw2': -3, 'fac': -3, 'qdafirst': True, 'sm': (-6, -5), 'rw2': (-4, -4), 'gat': (-5, -4), 'gfirst': False, 'out': (768, 384, 384), 'pin': {'gw': ('sT', -7, 1), 'gs': ('d3', -5, 3), 'w2s': ('d3', -3, 0), 'w13s': ('sT', 2, 2)}}
 K, T, E, C, H, N = 128, 1536, 6, 512, 512, 512
 SLOTS = E * C
 FLOPS = 2 * SLOTS * (N * H + 2 * H * K)
@@ -114,7 +114,7 @@ def tile_moe_bdx_glu_sigmoid_kernel(
             nc.vector.quantize_mx(t["w2c", e][:].bitcast(E4M3), t["w2s", e][:], t["w2b", e])
 
         def round_w13(e):
-            if O["c13"] == "G":
+            if O["c13"][e] == "G":
                 t["w13b", e] = t["sm", e][:, 0, :].bitcast(BF16)
                 for which in range(2):
                     nc.gpsimd.tensor_scalar(
@@ -129,7 +129,7 @@ def tile_moe_bdx_glu_sigmoid_kernel(
                 t["w13b", e] = work.tile([P, 2 * K * PACK], BF16, name="w13_bf16", align_bytes=64, bufs=O["w13b"])[:]
                 a = t["w13b", e].rearrange("p (w c i j) -> p w c j i", w=2, i=4, j=PACK)
                 b = t["w13", e][:].rearrange("p w j (c i) -> p w c j i", i=4)
-                if O["c13"] == "S":
+                if O["c13"][e] == "S":
                     nc.scalar.copy(a, b)
                 else:
                     nc.vector.tensor_copy(a, b)
@@ -203,6 +203,11 @@ def tile_moe_bdx_glu_sigmoid_kernel(
             t["C", g] = psum.tile([P, PACK, CHUNK], F32, name="da3_back", bufs=O["ps"][2])
             for j in range(PACK):
                 nc.tensor.transpose(t["C", g][:, j, :], t["d3T", g][:, j, :], identity[:])
+            t["C2", g] = t["C", g]
+            if g in O["dup"]:
+                t["C2", g] = psum.tile([P, PACK, CHUNK], F32, name="da3_again", tag=O["duptag"], bufs=dict(again=O["dupb"], a1_turned=O["ps"][0], da3_back=O["ps"][2])[O["duptag"]])
+                for j in range(PACK):
+                    nc.tensor.transpose(t["C2", g][:, j, :], t["d3T", g][:, j, :], identity[:])
 
         def round_da1(g):
             e, cols = where(g)
@@ -221,7 +226,7 @@ def tile_moe_bdx_glu_sigmoid_kernel(
 
         def round_da3(g):
             e, cols = where(g)
-            nc.scalar.copy(t["da", e][:, 1, cols, :], t["C", g][:].rearrange("p j c -> p c j"))
+            nc.scalar.copy(t["da", e][:, 1, cols, :], t["C2", g][:].rearrange("p j c -> p c j"))
 
         def quantize_da(e, first, last):
             if first == 0:
@@ -284,7 +289,7 @@ def tile_moe_bdx_glu_sigmoid_kernel(
         nc.tensor.transpose(gate_turned[:, 0:P], gate_rows[:], identity[:])
         nc.vector.tensor_copy(gate_cols[:], gate_turned[:, 0:CHUNKS])
 
-        order = sorted(((k, e) for e in range(E) for k in "wabx" if (k, e) not in done), key=lambda x: 4 * x[1] + O["lead"][x[0]])
+        order = sorted(((k, e) for e in range(E) for k in "wabx" if (k, e) not in done), key=lambda x: 4 * x[1] + O["lead"][x[0]] + O["slope"].get(x[0], 0) * x[1])
 
         def live(g):
             return 0 <= g < CHUNKS
@@ -296,19 +301,31 @@ def tile_moe_bdx_glu_sigmoid_kernel(
             if s == O["pos"]:
                 nc.sync.dma_start(first_list[:], pos1)
                 nc.sync.dma_start(second_list[:], pos2)
-            if live(s - 1):
-                turn_da3(s - 1)
-            if live(s + O["la"]):
-                turn_a1(s + O["la"])
-            if live(s + 1):
-                multiply_w2(s + 1)
-            if live(s):
-                da3_turned(s)
-            if live(s + O["la"]):
-                sigmoid_turned(s + O["la"])
-            if live(s - 1):
-                round_da1(s - 1)
-                round_da3(s - 1)
+            if O["pair"]:
+                if s % 2 == 0:
+                    la = 2 * ((O["la"] + 1) // 2)
+                    for fn, first in ((turn_da3, s - 2), (turn_a1, s + la), (da3_turned, s), (multiply_w2, s + 2), (sigmoid_turned, s + la)):
+                        for g in (first, first + 1):
+                            if live(g):
+                                fn(g)
+                    for g in (s - 2, s - 1):
+                        if live(g):
+                            round_da1(g)
+                            round_da3(g)
+            else:
+                if live(s - 1):
+                    turn_da3(s - 1)
+                if live(s + O["la"]):
+                    turn_a1(s + O["la"])
+                if live(s + O["lm"]):
+                    multiply_w2(s + O["lm"])
+                if live(s):
+                    da3_turned(s)
+                if live(s + O["la"]):
+                    sigmoid_turned(s + O["la"])
+                if live(s - 1):
+                    round_da1(s - 1)
+                    round_da3(s - 1)
             if s == CHUNKS - 1:
                 quantize_da(E - 1, 0, 2 * CHUNK)
             if s == CHUNKS:
@@ -324,7 +341,7 @@ def tile_moe_bdx_glu_sigmoid_kernel(
                 r = s - PER_EXPERT * e
                 if r == O["q13"]:
                     quantize_w13(e)
-                if r == O["r13"] and O["c13"] != "G":
+                if r == O["r13"] and O["c13"][e] != "G":
                     round_w13(e)
                 for half in range(len(O["sm"])):
                     if r == O["sm"][half]:
@@ -348,7 +365,7 @@ def tile_moe_bdx_glu_sigmoid_kernel(
                 parts = [q for q in range(O["un"]) if r == O["fac"] + q * O["fstep"]]
                 if parts:
                     factor(e, parts)
-                    if O["c13"] == "G" and O["un"] - 1 in parts:
+                    if O["c13"][e] == "G" and O["un"] - 1 in parts:
                         round_w13(e)
                 if r == O["gat"][0] and not O["gfirst"]:
                     gather_words(e)

from contextlib import ExitStack

import concourse.mybir as mybir
from concourse.masks import make_identity

O = {'slope': {}, 'dup': (23,), 'duptag': 'da3_back', 'dupb': 2, 'pair': False, 'lm': 1, 'fstep': 0, 'dtag': 'dx_sums', 'smb': 2, 'la': 2, 'addG': False, 'gw': 2, 'gs': 3, 'c13': 'SSSSSS', 'w13b': 1, 'w13c': 2, 'w2c': 1, 'w2b': 2, 'ub': 3, 'host': 'da', 'w2V': ((0, 1), (1, 0), (2, 0), (4, 0), (5, 1)), 'ps': (2, 2, 3), 'sT': 3, 'd3': 2, 'un': 4, 'uV': ((0, 0), (0, 3), (1, 1), (1, 3), (2, 1), (2, 2), (2, 3), (5, 1)), 'scq': 'Q', 'head': 'offs words scales a1 w2 gate', 'lead': {'w': 0, 'a': 1, 'b': 2, 'x': 5.5}, 'pos': 6, 'q13': 4, 'r13': 2, 'qw2': -3, 'fac': -3, 'qdafirst': True, 'sm': (-6, -5), 'rw2': (-4, -4), 'gat': (-5, -4), 'gfirst': False, 'out': (768, 384, 384), 'pin': {'gw': ('sT', -7, 1), 'gs': ('d3', -5, 3), 'w2s': ('d3', -3, 0), 'w13s': ('sT', 2, 2)}}
K, T, E, C, H, N = 128, 1536, 6, 512, 512, 512
SLOTS = E * C
FLOPS = 2 * SLOTS * (N * H + 2 * H * K)
BYTES = N * T + 16 * T + 4 * (2 * H * SLOTS + E * N * H + 2 * E * H * K + SLOTS + K * T) + 2 * 128 * (SLOTS + 2 * T) // 16

F32 = mybir.dt.float32
BF16 = mybir.dt.bfloat16
I32 = mybir.dt.int32
U32 = mybir.dt.uint32
U16 = mybir.dt.uint16
U8 = mybir.dt.uint8
E4M3 = mybir.dt.float8_e4m3fn_x4
E5M2 = mybir.dt.float8_e5m2_x4
MULT = mybir.AluOpType.mult
ADD = mybir.AluOpType.add
SIGMOID = mybir.ActivationFunctionType.Sigmoid

P = 128
PACK = 4
CHUNK = 128
HALF = 256
PER_EXPERT = C // CHUNK
CHUNKS = SLOTS // CHUNK
OUT_PIECES = O["out"]


def tile_moe_bdx_glu_sigmoid_kernel(
    tc, dy_words, dy_scales, a1, a3, w2, w1, w3, gate, offs, pos1, pos2, out
):
    nc = tc.nc
    with ExitStack() as ctx:
        held = ctx.enter_context(tc.tile_pool(name="held", bufs=1))
        loads = ctx.enter_context(tc.tile_pool(name="loads", bufs=3))
        work = ctx.enter_context(tc.tile_pool(name="work", bufs=2))
        ring = ctx.enter_context(tc.tile_pool(name="ring", bufs=3))
        psum = ctx.enter_context(tc.psum_pool(name="psum", bufs=2))

        slot_list = held.tile([P, SLOTS // 16], U16, name="slot_list")
        first_list = held.tile([P, T // 16], U16, name="first_list")
        second_list = held.tile([P, T // 16], U16, name="second_list")
        token_words = held.tile([P, T], I32, name="token_words", align_bytes=64)
        token_scales = held.tile([P, T], U8, name="token_scales", align_bytes=64)
        identity = held.tile([P, P], F32, name="identity")
        gate_rows = held.tile([P, P], F32, name="gate_rows")
        gate_cols = held.tile([P, CHUNKS], F32, name="gate_cols")
        dx = held.tile([P, SLOTS], F32, name="dx")

        t = {}
        pins = {}
        for kind, (src, r, first) in O["pin"].items():
            for e in range(first, E):
                if 0 <= PER_EXPERT * e + r < CHUNKS:
                    pins[src, PER_EXPERT * e + r] = (kind, e)
        pinned = set(pins.values())

        def place(pool, shape, dtype, name, key, bufs):
            if key in pins:
                key = pins[key]
            if key in pinned:
                return held.tile(shape, dtype, name=name, tag="pin_%s%d" % (key[0], key[1] % (3 if key[0] in ("gw", "gs") else 2)), align_bytes=64)
            return pool.tile(shape, dtype, name=name, align_bytes=64, bufs=bufs)

        def load_a1(e, first=0, last=C):
            if first == 0:
                t["a1", e] = loads.tile([P, PACK, C], F32, name="a1_rows")
            rows = a1[:, e * C + first : e * C + last].rearrange("(p j) c -> p j c", j=PACK)
            nc.sync.dma_start(t["a1", e][:, :, first:last], rows)

        def load_a3(e):
            t["a3", e] = loads.tile([P, PACK, C], F32, name="a3_rows")
            nc.sync.dma_start(t["a3", e][:], a3[:, e * C : (e + 1) * C].rearrange("(p j) c -> p j c", j=PACK))

        def load_w2(e, first=0, last=H):
            if first == 0:
                t["w2", e] = loads.tile([P, PACK, H], F32, name="w2_rows")
            nc.sync.dma_start(t["w2", e][:, :, first:last], w2[e][:, first:last].rearrange("(p j) i -> p j i", j=PACK))

        def load_w13(e):
            t["w13", e] = loads.tile([P, 2, PACK, K], F32, name="w13_rows")
            for which, w in enumerate((w1, w3)):
                nc.sync.dma_start(t["w13", e][:, which], w[e].rearrange("(p j) k -> p j k", j=PACK))

        def gather_words(e):
            t["gw", e] = place(work, [P, C], U32, "slot_words", ("gw", e), O["gw"])
            nc.vector.tensor_copy(
                t["gw", e][:], token_words[:].bitcast(U32).indirect(slot_list[:, e * C // 16 : (e + 1) * C // 16])
            )

        def gather_scales(e):
            t["gs", e] = place(work, [P, C], U8, "slot_scales", ("gs", e), O["gs"])
            nc.vector.tensor_copy(t["gs", e][:], token_scales[:].indirect(slot_list[:, e * C // 16 : (e + 1) * C // 16]))

        def round_w2(e, half):
            if half == 0 and O["host"] == "w2":
                t["u", e] = work.tile([P, PACK, C], F32, name="w2_then_factor", align_bytes=64, bufs=3)
                t["w2b", e] = t["u", e][:, 0:2, :].rearrange("p j c -> p (j c)").bitcast(BF16)
            elif half == 0:
                t["w2b", e] = work.tile([P, H * PACK], BF16, name="w2_bf16", align_bytes=64, bufs=O["w2b"])[:]
            staged = t["w2b", e].rearrange("p (c i j) -> p c j i", i=4, j=PACK)
            (nc.vector.tensor_copy if (e, half) in O["w2V"] else nc.scalar.copy)(
                staged[:, half * (128 // len(O["rw2"])) : (half + 1) * (128 // len(O["rw2"]))],
                t["w2", e][:, :, half * (H // len(O["rw2"])) : (half + 1) * (H // len(O["rw2"]))].rearrange("p j (c i) -> p c j i", i=4),
            )

        def quantize_w2(e):
            t["w2c", e] = work.tile([P, H], U32, name="w2_codes", align_bytes=64, bufs=O["w2c"])
            t["w2s", e] = place(work, [P, H], U8, "w2_scales", ("w2s", e), O["w2c"])
            nc.vector.quantize_mx(t["w2c", e][:].bitcast(E4M3), t["w2s", e][:], t["w2b", e])

        def round_w13(e):
            if O["c13"][e] == "G":
                t["w13b", e] = t["sm", e][:, 0, :].bitcast(BF16)
                for which in range(2):
                    nc.gpsimd.tensor_scalar(
                        t["w13b", e][:, which * C : (which + 1) * C].rearrange("p (k j) -> p k j", j=PACK),
                        t["w13", e][:, which].rearrange("p j k -> p k j"),
                        1.0,
                        0.0,
                        MULT,
                        ADD,
                    )
            else:
                t["w13b", e] = work.tile([P, 2 * K * PACK], BF16, name="w13_bf16", align_bytes=64, bufs=O["w13b"])[:]
                a = t["w13b", e].rearrange("p (w c i j) -> p w c j i", w=2, i=4, j=PACK)
                b = t["w13", e][:].rearrange("p w j (c i) -> p w c j i", i=4)
                if O["c13"][e] == "S":
                    nc.scalar.copy(a, b)
                else:
                    nc.vector.tensor_copy(a, b)

        def quantize_w13(e):
            t["w13c", e] = work.tile([P, 2 * K], U32, name="w13_codes", align_bytes=64, bufs=O["w13c"])
            t["w13s", e] = place(work, [P, 2 * K], U8, "w13_scales", ("w13s", e), O["w13c"])
            nc.vector.quantize_mx(t["w13c", e][:].bitcast(E4M3), t["w13s", e][:], t["w13b", e])

        def where(g):
            e, c = divmod(g, PER_EXPERT)
            return e, slice(c * CHUNK, (c + 1) * CHUNK)

        def turn_a1(g):
            e, cols = where(g)
            t["A", g] = psum.tile([P, PACK, P], F32, name="a1_turned", bufs=O["ps"][0])
            for j in range(PACK):
                nc.tensor.transpose(t["A", g][:, j, :], t["a1", e][:, j, cols], identity[:])

        def multiply_w2(g):
            e, cols = where(g)
            t["B", g] = psum.tile([P, H], F32, name="dh_sums", bufs=O["ps"][1])
            nc.tensor.matmul_mx(
                t["B", g][:],
                lhsT=t["gw", e][:, cols].bitcast(E5M2),
                lhsT_scale=t["gs", e][:, cols],
                rhs=t["w2c", e][:].bitcast(E4M3),
                rhs_scale=t["w2s", e][:],
                start=True,
                stop=True,
            )

        def sigmoid_turned(g):
            t["sT", g] = place(ring, [P, PACK, P], F32, "sig_turned", ("sT", g), O["sT"])
            nc.scalar.activation(t["sT", g][:], t["A", g][:], SIGMOID)

        def sigmoid_negated(e, half):
            if half == 0:
                t["sm", e] = work.tile([P, PACK, C], F32, name="sig_negated", align_bytes=64, bufs=O["smb"])
            cols = slice(half * (C // len(O["sm"])), (half + 1) * (C // len(O["sm"])))
            nc.scalar.activation(t["sm", e][:, :, cols], t["a1", e][:, :, cols], SIGMOID, scale=-1.0)

        def factor(e, parts):
            n = O["un"]
            if 0 not in parts:
                pass
            elif O["host"] == "da":
                if e < 2:
                    t["u", e] = held.tile([P, PACK, C], F32, name="da_then_factor", tag="zone%d" % ((e - 2) % 3), align_bytes=64)
                else:
                    t["u", e] = t["Z", e - 2]
            elif O["host"] == "none":
                t["u", e] = work.tile([P, PACK, C], F32, name="factor", align_bytes=64, bufs=O["ub"])
            for part in parts:
                cols = slice(part * C // n, (part + 1) * C // n)
                eng = nc.vector if (e, part) in O["uV"] else nc.gpsimd
                eng.tensor_tensor(t["u", e][:, :, cols], t["sm", e][:, :, cols], t["a3", e][:, :, cols], MULT)

        def da3_turned(g):
            t["d3T", g] = place(ring, [P, PACK, P], F32, "da3_turned", ("d3", g), O["d3"])
            nc.vector.scalar_tensor_tensor(
                t["d3T", g][:],
                t["B", g][:].rearrange("p (m j) -> p j m", j=PACK),
                gate_cols[:, g : g + 1],
                t["sT", g][:],
                MULT,
                MULT,
            )

        def turn_da3(g):
            t["C", g] = psum.tile([P, PACK, CHUNK], F32, name="da3_back", bufs=O["ps"][2])
            for j in range(PACK):
                nc.tensor.transpose(t["C", g][:, j, :], t["d3T", g][:, j, :], identity[:])
            t["C2", g] = t["C", g]
            if g in O["dup"]:
                t["C2", g] = psum.tile([P, PACK, CHUNK], F32, name="da3_again", tag=O["duptag"], bufs=dict(again=O["dupb"], a1_turned=O["ps"][0], da3_back=O["ps"][2])[O["duptag"]])
                for j in range(PACK):
                    nc.tensor.transpose(t["C2", g][:, j, :], t["d3T", g][:, j, :], identity[:])

        def round_da1(g):
            e, cols = where(g)
            if g % PER_EXPERT == 0:
                if O["host"] == "da":
                    t["Z", e] = held.tile([P, PACK, C], F32, name="da_then_factor", tag="zone%d" % (e % 3), align_bytes=64)
                    t["da", e] = t["Z", e][:].rearrange("p j c -> p (j c)").bitcast(BF16).rearrange("p (w c j) -> p w c j", w=2, j=PACK)
                else:
                    t["da", e] = work.tile([P, 2, C, PACK], BF16, name="da_bf16", align_bytes=64)
            nc.vector.tensor_tensor(
                t["da", e][:, 0, cols, :].rearrange("p (c i) j -> p c j i", i=2),
                t["C", g][:].rearrange("p j (c i) -> p c j i", i=2),
                t["u", e][:, :, cols].rearrange("p j (c i) -> p c j i", i=2),
                MULT,
            )

        def round_da3(g):
            e, cols = where(g)
            nc.scalar.copy(t["da", e][:, 1, cols, :], t["C2", g][:].rearrange("p j c -> p c j"))

        def quantize_da(e, first, last):
            if first == 0:
                t["dac", e] = work.tile([P, 2 * C], U32, name="da_codes", align_bytes=64)
                t["das", e] = work.tile([P, 2 * C], U8, name="da_scales", align_bytes=64)
            if last - first == C:
                nc.vector.quantize_mx(t["dac", e][:].bitcast(E5M2), t["das", e][:], t["da", e][:].rearrange("p w c j -> p (w c j)"))
                return
            for which in range(2):
                part = slice(which * C + first, which * C + last)
                nc.vector.quantize_mx(
                    t["dac", e][:, part].bitcast(E5M2),
                    t["das", e][:, part],
                    t["da", e][:, which, first:last, :].rearrange("p c j -> p (c j)"),
                )

        def multiply_w13(e):
            t["D", e] = psum.tile([P, C], F32, name="dx_sums", tag=O["dtag"], bufs=dict(dx_sums=1, a1_turned=O["ps"][0], dh_sums=O["ps"][1], da3_back=O["ps"][2])[O["dtag"]])
            for which in range(2):
                kcols = slice(which * K, (which + 1) * K)
                half = slice(which * C, (which + 1) * C)
                nc.tensor.matmul_mx(
                    t["D", e][:],
                    lhsT=t["w13c", e][:, kcols].bitcast(E4M3),
                    lhsT_scale=t["w13s", e][:, kcols],
                    rhs=t["dac", e][:, half].bitcast(E5M2),
                    rhs_scale=t["das", e][:, half],
                    start=(which == 0),
                    stop=(which == 1),
                )

        def keep_dx(e):
            nc.scalar.copy(dx[:, e * C : (e + 1) * C], t["D", e][:])

        make_identity(nc, identity[:])
        nc.vector.memset(token_scales[:].bitcast(I32), 0)
        def load_scales():
            for q in range(4):
                (nc.scalar if O["scq"] == "S" else nc.sync).dma_start(token_scales[32 * q : 32 * q + 4, :].bitcast(I32), dy_scales[0, 4 * q : 4 * q + 4, :].bitcast(I32))

        head = dict(
            offs=lambda: nc.sync.dma_start(slot_list[:], offs),
            words=lambda: nc.sync.dma_start(token_words[:], dy_words[0].rearrange("p t d -> p (t d)").bitcast(I32)),
            scales=load_scales,
            a1a=lambda: load_a1(0, 0, HALF),
            a1b=lambda: load_a1(0, HALF, C),
            a1=lambda: load_a1(0),
            w2a=lambda: load_w2(0, 0, HALF),
            w2b=lambda: load_w2(0, HALF, H),
            w2=lambda: load_w2(0),
            gate=lambda: nc.sync.dma_start(gate_rows[:], gate.rearrange("h (r c) -> (h r) c", c=P)[0:P, :]),
            a3=lambda: load_a3(0),
            w13=lambda: load_w13(0),
        )
        done = set()
        for key in O["head"].split():
            head[key]()
            done.add((dict(a1="a", a1a="a", w2="w", w2a="w", a3="b", w13="x").get(key), 0))
        gate_turned = psum.tile([P, C], F32, name="dx_sums", tag=O["dtag"], bufs=dict(dx_sums=1, a1_turned=O["ps"][0], dh_sums=O["ps"][1], da3_back=O["ps"][2])[O["dtag"]])
        nc.tensor.transpose(gate_turned[:, 0:P], gate_rows[:], identity[:])
        nc.vector.tensor_copy(gate_cols[:], gate_turned[:, 0:CHUNKS])

        order = sorted(((k, e) for e in range(E) for k in "wabx" if (k, e) not in done), key=lambda x: 4 * x[1] + O["lead"][x[0]] + O["slope"].get(x[0], 0) * x[1])

        def live(g):
            return 0 <= g < CHUNKS

        for s in range(-12, CHUNKS + 3):
            if s + 12 < len(order):
                kind, e_load = order[s + 12]
                dict(a=load_a1, w=load_w2, b=load_a3, x=load_w13)[kind](e_load)
            if s == O["pos"]:
                nc.sync.dma_start(first_list[:], pos1)
                nc.sync.dma_start(second_list[:], pos2)
            if O["pair"]:
                if s % 2 == 0:
                    la = 2 * ((O["la"] + 1) // 2)
                    for fn, first in ((turn_da3, s - 2), (turn_a1, s + la), (da3_turned, s), (multiply_w2, s + 2), (sigmoid_turned, s + la)):
                        for g in (first, first + 1):
                            if live(g):
                                fn(g)
                    for g in (s - 2, s - 1):
                        if live(g):
                            round_da1(g)
                            round_da3(g)
            else:
                if live(s - 1):
                    turn_da3(s - 1)
                if live(s + O["la"]):
                    turn_a1(s + O["la"])
                if live(s + O["lm"]):
                    multiply_w2(s + O["lm"])
                if live(s):
                    da3_turned(s)
                if live(s + O["la"]):
                    sigmoid_turned(s + O["la"])
                if live(s - 1):
                    round_da1(s - 1)
                    round_da3(s - 1)
            if s == CHUNKS - 1:
                quantize_da(E - 1, 0, 2 * CHUNK)
            if s == CHUNKS:
                quantize_da(E - 1, 2 * CHUNK, 3 * CHUNK)
            for e in range(E):
                r = s - PER_EXPERT * e
                if r == 5 and O["qdafirst"]:
                    quantize_da(e, 3 * CHUNK if e == E - 1 else 0, C)
                    multiply_w13(e)
                if r == 6:
                    keep_dx(e)
            for e in range(E):
                r = s - PER_EXPERT * e
                if r == O["q13"]:
                    quantize_w13(e)
                if r == O["r13"] and O["c13"][e] != "G":
                    round_w13(e)
                for half in range(len(O["sm"])):
                    if r == O["sm"][half]:
                        sigmoid_negated(e, half)
                for half in range(len(O["rw2"])):
                    if r == O["rw2"][half]:
                        round_w2(e, half)
                if r == O["gat"][0] and O["gfirst"]:
                    gather_words(e)
                if r == O["gat"][1] and O["gfirst"]:
                    gather_scales(e)
                if r == O["qw2"]:
                    quantize_w2(e)
            for e in range(E):
                r = s - PER_EXPERT * e
                if r == 5 and not O["qdafirst"]:
                    quantize_da(e, 3 * CHUNK if e == E - 1 else 0, C)
                    multiply_w13(e)
            for e in range(E):
                r = s - PER_EXPERT * e
                parts = [q for q in range(O["un"]) if r == O["fac"] + q * O["fstep"]]
                if parts:
                    factor(e, parts)
                    if O["c13"][e] == "G" and O["un"] - 1 in parts:
                        round_w13(e)
                if r == O["gat"][0] and not O["gfirst"]:
                    gather_words(e)
                if r == O["gat"][1] and not O["gfirst"]:
                    gather_scales(e)

        start = 0
        for width in OUT_PIECES:
            cols = slice(start // 16, (start + width) // 16)
            first = work.tile([P, width], F32, name="first")
            second = work.tile([P, width], F32, name="second")
            total = work.tile([P, width], F32, name="total", bufs=3)
            nc.vector.tensor_copy(first[:], dx[:].indirect(first_list[:, cols]))
            nc.vector.tensor_copy(second[:], dx[:].indirect(second_list[:, cols]))
            (nc.gpsimd if O["addG"] and start + width < T else nc.vector).tensor_tensor(total[:], first[:], second[:], ADD)
            nc.sync.dma_start(out[:, start : start + width], total[:])
            start += width
